import numpy as np
import ml_dtypes


def mxq(x, axis, fmt="e4m3"):
    dtype, down = {"e4m3": (ml_dtypes.float8_e4m3fn, 7), "e5m2": (ml_dtypes.float8_e5m2, 14)}[fmt]
    v = np.moveaxis(np.asarray(x, np.float32).astype(ml_dtypes.bfloat16).astype(np.float64), axis, -1)
    blocks = v.reshape(v.shape[:-1] + (-1, 32))
    amax = np.abs(blocks).max(-1, keepdims=True)
    byte = np.maximum(np.where(amax > 0, np.frexp(amax)[1] - 1 + 127, 0) - down, 1)
    scale = np.exp2(byte - 127.0)
    codes = (blocks / scale).astype(np.float32).astype(dtype).astype(np.float64)
    return np.moveaxis((codes * scale).reshape(v.shape), -1, axis)


WIDE = False


def mx_kscale(k):
    if not WIDE:
        return np.ones(k)
    levels = np.array([24, -24, 12, -12, 0])
    if k % 512:
        return np.exp2(np.random.permutation(np.resize(levels, k // 32))).repeat(32)
    a = np.empty((k // 512, 16))
    for p in range(k // 512):
        a[p, :8] = np.random.permutation(np.resize(levels, 8))
        for g in range(8):
            far = levels[np.abs(levels - a[p, g]) >= 10]
            a[p, g + 8] = far[np.random.randint(len(far))]
    return np.exp2(a.ravel()).repeat(32)


def f64(x):
    return np.asarray(x).astype(np.float64)


def striped(idx):
    return np.tile(idx.reshape(-1, 16).T, (8, 1)).astype(np.uint16)


def unstriped(offs):
    return offs[:16].T.reshape(-1).astype(np.int64)


def striped8(idx):
    return np.concatenate([v.reshape(-1, 16).T for v in idx]).astype(np.uint16)


def unstriped8(offs):
    return np.stack([offs[16 * g:16 * g + 16].T.reshape(-1) for g in range(8)]).astype(np.int64)


E2M1 = np.array([0.0, 0.5, 1.0, 1.5, 2.0, 3.0, 4.0, 6.0, -0.0, -0.5, -1.0, -1.5, -2.0, -3.0, -4.0, -6.0])


def pack_weight(w, fmt):
    k, n = w.shape
    w = f64(np.asarray(w, np.float32).astype(ml_dtypes.bfloat16)).reshape(k // 32, 32, n)
    amax = np.abs(w).max(1)
    if fmt == "e4m3":
        byte = np.frexp(amax)[1] - 1 + 127 - 7
    else:
        mant, ex = np.frexp(amax / 6.0)
        byte = np.where(mant > 0.5, ex, ex - 1) + 127
    byte = np.clip(np.where(amax > 0, byte, 1), 1, 254)
    scaled = (w * np.exp2(127.0 - byte)[:, None, :]).reshape(k, n).astype(np.float32)
    by_word = np.ascontiguousarray(scaled.reshape(k // 512, 128, 4, n).transpose(0, 1, 3, 2))
    if fmt == "e4m3":
        words = by_word.astype(ml_dtypes.float8_e4m3fn).view(np.uint8)
    else:
        c = by_word.astype(ml_dtypes.float4_e2m1fn).view(np.uint8) & 0xF
        words = (c[..., 0::2] | (c[..., 1::2] << 4)).reshape(k // 512, 128, 2 * n)
    return np.ascontiguousarray(words), np.ascontiguousarray(byte.astype(np.uint8).reshape(k // 512, 16, n))


def unpack_weight(words, scales, fmt):
    g, _, n = scales.shape
    words = np.ascontiguousarray(words).reshape(g, 128, n, -1)
    if fmt == "e4m3":
        vals = words.view(ml_dtypes.float8_e4m3fn).astype(np.float64)
    else:
        nib = np.empty((g, 128, n, 4), np.uint8)
        nib[..., 0::2] = words & 0xF
        nib[..., 1::2] = words >> 4
        vals = E2M1[nib]
    vals = vals * np.repeat(np.exp2(scales.astype(np.float64) - 127.0), 8, axis=1)[..., None]
    return vals.transpose(0, 1, 3, 2).reshape(g * 512, n)


def planes(y):
    n, m = y.shape
    v = y.astype(np.float32).astype(ml_dtypes.bfloat16).astype(np.float64).reshape(n // 32, 32, m)
    top = np.abs(v).max(1)
    byte = np.clip(np.where(top > 0, np.frexp(top)[1] - 1 + 127 - 7, 1), 1, 254)
    codes = (v * np.exp2(127.0 - byte)[:, None, :]).reshape(n, m).astype(np.float32).astype(ml_dtypes.float8_e4m3fn).view(np.uint8)
    words = codes.reshape(n // 512, 128, 4, m).transpose(0, 1, 3, 2)
    return np.ascontiguousarray(words), np.ascontiguousarray(byte.astype(np.uint8).reshape(n // 512, 16, m))


K, L, R, N, T, J = 512, 512, 512, 512, 2048, 1024


def setup_inputs():
    n = np.random.standard_normal
    s = mx_kscale(K)[:, None]
    s2 = mx_kscale(L)[:, None]
    u = mx_kscale(R)[:, None]
    p_tab = pack_weight(n((L, T)) * s2, "e4m3")
    p_wb = pack_weight(n((L, R)) / np.sqrt(L) / s2 * u.T, "e4m3")
    return {
        "tab_words": p_tab[0],
        "tab_scales": p_tab[1],
        "xT": (n((K, T)) * s).astype(np.float32),
        "wgt2": np.repeat(np.random.uniform(0.5, 2.0, (8, J)), 16, axis=0).astype(np.float32),
        "wa": (n((K, R)) / np.sqrt(K) / s * u.T).astype(np.float32),
        "wb_words": p_wb[0],
        "wb_scales": p_wb[1],
        "wd": (n((R, N)) / np.sqrt(R) / u).astype(np.float32),
        "res": (n((N, J))).astype(np.float32),
        "offs": striped(np.random.permutation(T)[:J]),
        "offs2": striped8(np.stack([np.random.permutation(T)[:J] for _ in range(8)])),
    }


def reference(tab_words, tab_scales, xT, wgt2, wa, wb_words, wb_scales, wd, res, offs, offs2):
    idx = unstriped(offs)
    idx2 = unstriped8(offs2)
    tab_ = unpack_weight(tab_words, tab_scales, "e4m3")[:, idx]
    rows = np.arange(K)
    xg = f64(wgt2)[rows // 4 % 128] * f64(xT)[rows[:, None], idx2[rows % 512 // 64]]
    xT_ = mxq(xg, 0, "e4m3")
    wa_ = mxq(f64(wa), 0, "e4m3")
    wb_ = unpack_weight(wb_words, wb_scales, "e4m3")
    ya = wa_.T @ xT_
    yb = wb_.T @ tab_
    h = np.maximum(ya, yb)
    h_ = mxq(h, 0, "e4m3")
    wd_ = mxq(f64(wd), 0, "e4m3")
    y = wd_.T @ h_
    out_0 = f64(res) + y
    return (out_0,) + planes(out_0)

@@ -1,0 +1,205 @@
+from contextlib import ExitStack
+
+import concourse.mybir as mybir
+
+K, L, R, N, T, J = 512, 512, 512, 512, 2048, 1024
+FLOPS = 2 * J * (K * R + L * R + R * N)
+
+F32 = mybir.dt.float32
+BF16 = mybir.dt.bfloat16
+I32 = mybir.dt.int32
+U32 = mybir.dt.uint32
+U16 = mybir.dt.uint16
+U8 = mybir.dt.uint8
+FP8X4 = mybir.dt.float8_e4m3fn_x4
+ALU = mybir.AluOpType
+
+P = 128
+PACK = 4
+BANK_COLS = 128
+GROUP = 256
+GROUPS = J // GROUP
+PER_COL = 16
+
+
+def tile_list_htabg_max_resP_kernel(
+    tc, tab_words, tab_scales, xT, wgt2, wa, wb_words, wb_scales, wd, res, offs, offs2, out_0, out_1, out_2
+):
+    nc = tc.nc
+    with ExitStack() as ctx:
+        keep = ctx.enter_context(tc.tile_pool(name="keep", bufs=1))
+        psum = ctx.enter_context(tc.psum_pool(name="psum", bufs=1))
+
+        def sb(name, shape, dtype):
+            return keep.tile(shape, dtype, name=name, align_bytes=64)
+
+        def words_of(dram):
+            return dram[0].rearrange("p c i -> p (c i)").bitcast(I32)
+
+        def quantize(codes, scales, values):
+            nc.vector.quantize_mx(out=codes.bitcast(FP8X4), scales=scales, in_=values)
+
+        def project(bank, w_codes, w_scales, codes, scales):
+            for t in range(PACK):
+                cols = slice(t * P, (t + 1) * P)
+                nc.tensor.matmul_mx(
+                    out=bank[:, t, :],
+                    lhsT=w_codes[:, cols].bitcast(FP8X4),
+                    lhsT_scale=w_scales[:, cols],
+                    rhs=codes.bitcast(FP8X4),
+                    rhs_scale=scales,
+                    start=True,
+                    stop=True,
+                )
+
+        tab_list = keep.tile([P, J // PER_COL], U16, name="tab_list")
+        head_lists = keep.tile([P, J // PER_COL], U16, name="head_lists")
+        tab_w = sb("tab_w", [P, T], I32)
+        tab_s = sb("tab_s", [P, T], U8)
+        wb_w = sb("wb_w", [P, R], I32)
+        wb_s = sb("wb_s", [P, R], U8)
+        wgt = sb("wgt", [P, J], F32)
+        x_planes = [sb("x%d" % i, [P, T], F32) for i in range(PACK)]
+        wa_raw = [sb("wa_raw%d" % h, [P, PACK, R // 2], F32) for h in range(2)]
+        wd_raw = sb("wd_raw", [P, PACK, N], F32)
+        res_sb = [sb("res%d" % g, [P, PACK, GROUP], F32) for g in range(GROUPS)]
+
+        nc.vector.memset(wb_s[:].bitcast(I32), 0)
+
+        x_rows = xT.rearrange("(p i) t -> p i t", i=PACK)
+        wa_rows = wa.rearrange("(p i) r -> p i r", i=PACK)
+        res_rows = res.rearrange("(p t) j -> p t j", t=PACK)
+        out_rows = out_0.rearrange("(p t) j -> p t j", t=PACK)
+
+        nc.sync.dma_start(tab_list[:], offs)
+        for q in range(4):
+            rows = tab_scales[0, 4 * q : 4 * q + 4, :].bitcast(I32)
+            nc.sync.dma_start(tab_s[32 * q : 32 * q + 32, :].bitcast(I32), rows.partition_broadcast(8))
+        nc.sync.dma_start(tab_w[:], words_of(tab_words))
+        nc.sync.dma_start(wb_w[:], words_of(wb_words))
+        nc.sync.dma_start(head_lists[:], offs2)
+        for q in range(4):
+            nc.sync.dma_start(wb_s[32 * q : 32 * q + 4, :].bitcast(I32), wb_scales[0, 4 * q : 4 * q + 4, :].bitcast(I32))
+        nc.sync.dma_start(wgt[:], wgt2)
+        for i in range(PACK):
+            nc.sync.dma_start(x_planes[i][:], x_rows[:, i, :])
+        for h in range(2):
+            nc.sync.dma_start(wa_raw[h][:], wa_rows[:, :, h * (R // 2) : (h + 1) * (R // 2)])
+        nc.sync.dma_start(wd_raw[:], wd.rearrange("(p i) n -> p i n", i=PACK))
+        for g in range(GROUPS):
+            nc.sync.dma_start(res_sb[g][:], res_rows[:, :, g * GROUP : (g + 1) * GROUP])
+
+        v_codes = sb("v_codes", [P, J], U32)
+        v_scales = sb("v_scales", [P, J], U8)
+        wb_codes = sb("wb_codes", [P, R], I32)
+        wb_sc = sb("wb_sc", [P, R], U8)
+        nc.vector.tensor_copy(v_scales[:], tab_s[:].indirect(tab_list[:]))
+        nc.vector.tensor_copy(v_codes[:], tab_w[:].bitcast(U32).indirect(tab_list[:]))
+        nc.vector.tensor_copy(wb_codes[:].rearrange("p (t m) -> p t m", t=PACK), wb_w[:].rearrange("p (m t) -> p t m", t=PACK))
+        nc.vector.tensor_copy(wb_sc[:].rearrange("p (t m) -> p t m", t=PACK), wb_s[:].rearrange("p (m t) -> p t m", t=PACK))
+
+        def bank_tile(b):
+            return psum.tile([P, PACK, BANK_COLS], F32, name="bank%d" % b)
+
+        yb = []
+        for c in range(J // BANK_COLS):
+            cols = slice(c * BANK_COLS, (c + 1) * BANK_COLS)
+            bank = bank_tile(4 + c % 4)
+            project(bank, wb_codes, wb_sc, v_codes[:, cols], v_scales[:, cols])
+            yb_c = sb("yb%d" % c, [P, BANK_COLS, PACK], F32)
+            nc.scalar.copy(yb_c[:], bank[:].rearrange("p t j -> p j t"))
+            yb.append(yb_c)
+
+        picked01 = sb("picked01", [P, 2, J], F32)
+        for i in range(2):
+            nc.vector.tensor_tensor(picked01[:, i, :], x_planes[i][:].indirect(head_lists[:]), wgt[:], ALU.mult)
+        xg = [sb("xg%d" % g, [P, GROUP, PACK], BF16) for g in range(GROUPS)]
+        picked23 = [sb("picked23_%d" % g, [P, 2, GROUP], F32) for g in range(GROUPS)]
+
+        def pick(i, g):
+            offsets = head_lists[:, g * GROUP // PER_COL : (g + 1) * GROUP // PER_COL]
+            nc.vector.tensor_tensor(
+                picked23[g][:, i - 2, :], x_planes[i][:].indirect(offsets), wgt[:, g * GROUP : (g + 1) * GROUP], ALU.mult
+            )
+
+        for g in range(GROUPS):
+            nc.scalar.copy(xg[g][:, :, 0:2], picked01[:, :, g * GROUP : (g + 1) * GROUP].rearrange("p i j -> p j i"))
+        for g in range(GROUPS):
+            pick(2, g)
+
+        wa_bf = sb("wa_bf", [P, PACK, P, PACK], BF16)
+        wd_bf = sb("wd_bf", [P, PACK, P, PACK], BF16)
+        wa_codes = sb("wa_codes", [P, R], U32)
+        wa_sc = sb("wa_sc", [P, R], U8)
+        wd_codes = sb("wd_codes", [P, N], U32)
+        wd_sc = sb("wd_sc", [P, N], U8)
+        out_codes = sb("out_codes", [P, J], U32)
+        out_sc = sb("out_sc", [P, J], U8)
+
+        def deal(copy, dst, src):
+            copy(dst.rearrange("p t m i -> p m i t"), src.rearrange("p i (m t) -> p m i t", t=PACK))
+
+        halves = GROUP // BANK_COLS
+        xg_q, h_q = {}, {}
+
+        def finish_picks(g):
+            pick(3, g)
+            nc.scalar.copy(xg[g][:, :, 2:4], picked23[g][:].rearrange("p i j -> p j i"))
+            xg_codes = sb("xg_codes%d" % g, [P, GROUP], U32)
+            xg_sc = sb("xg_sc%d" % g, [P, GROUP], U8)
+            quantize(xg_codes[:], xg_sc[:], xg[g][:].rearrange("p j i -> p (j i)"))
+            xg_q[g] = (xg_codes, xg_sc)
+
+        def first_layer(g):
+            xg_codes, xg_sc = xg_q[g]
+            h_bf = sb("h_bf%d" % g, [P, GROUP, PACK], BF16)
+            for u in range(halves):
+                cols = slice(u * BANK_COLS, (u + 1) * BANK_COLS)
+                bank = bank_tile(halves * (g % 2) + u)
+                project(bank, wa_codes, wa_sc, xg_codes[:, cols], xg_sc[:, cols])
+                nc.vector.tensor_tensor(h_bf[:, cols, :], bank[:].rearrange("p t j -> p j t"), yb[g * halves + u][:], ALU.max)
+            h_codes = sb("h_codes%d" % g, [P, GROUP], U32)
+            h_sc = sb("h_sc%d" % g, [P, GROUP], U8)
+            quantize(h_codes[:], h_sc[:], h_bf[:].rearrange("p j t -> p (j t)"))
+            h_q[g] = (h_codes, h_sc)
+
+        def second_layer(g):
+            gcols = slice(g * GROUP, (g + 1) * GROUP)
+            h_codes, h_sc = h_q[g]
+            out_sb = sb("out%d" % g, [P, PACK, GROUP], F32)
+            out_bf = sb("out_bf%d" % g, [P, GROUP, PACK], BF16)
+            for u in range(halves):
+                cols = slice(u * BANK_COLS, (u + 1) * BANK_COLS)
+                bank = bank_tile(halves * g + u)
+                project(bank, wd_codes, wd_sc, h_codes[:, cols], h_sc[:, cols])
+                nc.vector.tensor_tensor(out_sb[:, :, cols], bank[:], res_sb[g][:, :, cols], ALU.add)
+                last = g == GROUPS - 1 and u == halves - 1
+                copy = nc.vector.tensor_copy if last else nc.scalar.copy
+                copy(
+                    out_bf[:, cols, :].rearrange("p (c q) t -> p c t q", q=4),
+                    out_sb[:, :, cols].rearrange("p t (c q) -> p c t q", q=4),
+                )
+            nc.sync.dma_start(out_rows[:, :, gcols], out_sb[:])
+            quantize(out_codes[:, gcols], out_sc[:, gcols], out_bf[:].rearrange("p j t -> p (j t)"))
+            nc.sync.dma_start(words_of(out_1)[:, gcols], out_codes[:, gcols].bitcast(I32))
+
+        finish_picks(0)
+        deal(nc.scalar.copy, wa_bf[:, :, 0 : P // 2, :], wa_raw[0][:])
+        deal(nc.vector.tensor_copy, wa_bf[:, :, P // 2 : P, :], wa_raw[1][:])
+        quantize(wa_codes[:], wa_sc[:], wa_bf[:].rearrange("p t m i -> p (t m i)"))
+        finish_picks(1)
+        first_layer(0)
+        deal(nc.scalar.copy, wd_bf[:], wd_raw[:])
+        quantize(wd_codes[:], wd_sc[:], wd_bf[:].rearrange("p t m i -> p (t m i)"))
+        finish_picks(2)
+        first_layer(1)
+        finish_picks(3)
+        second_layer(0)
+        first_layer(2)
+        second_layer(1)
+        first_layer(3)
+        second_layer(2)
+        second_layer(3)
+        for q in range(4):
+            queue = nc.sync if q % 2 == 0 else nc.scalar
+            queue.dma_start(out_2[0, 4 * q : 4 * q + 4, :].bitcast(I32), out_sc[32 * q : 32 * q + 4, :].bitcast(I32))

@@ -19,6 +19,7 @@ PACK = 4
 BANK_COLS = 128
 GROUP = 256
 GROUPS = J // GROUP
+RUN = 8
 PER_COL = 16
 
 
@@ -85,7 +86,9 @@ def tile_list_htabg_max_resP_kernel(
             nc.sync.dma_start(x_planes[i][:], x_rows[:, i, :])
         for h in range(2):
             nc.sync.dma_start(wa_raw[h][:], wa_rows[:, :, h * (R // 2) : (h + 1) * (R // 2)])
-        nc.sync.dma_start(wd_raw[:], wd.rearrange("(p i) n -> p i n", i=PACK))
+        wd_rows = wd.rearrange("(b t u) n -> t b u n", t=PACK, u=RUN)
+        for t in range(PACK):
+            nc.sync.dma_start(wd_raw[:, t, :], wd_rows[t])
         for g in range(GROUPS):
             nc.sync.dma_start(res_sb[g][:], res_rows[:, :, g * GROUP : (g + 1) * GROUP])
 
@@ -95,8 +98,13 @@ def tile_list_htabg_max_resP_kernel(
         wb_sc = sb("wb_sc", [P, R], U8)
         nc.vector.tensor_copy(v_scales[:], tab_s[:].indirect(tab_list[:]))
         nc.vector.tensor_copy(v_codes[:], tab_w[:].bitcast(U32).indirect(tab_list[:]))
-        nc.vector.tensor_copy(wb_codes[:].rearrange("p (t m) -> p t m", t=PACK), wb_w[:].rearrange("p (m t) -> p t m", t=PACK))
-        nc.vector.tensor_copy(wb_sc[:].rearrange("p (t m) -> p t m", t=PACK), wb_s[:].rearrange("p (m t) -> p t m", t=PACK))
+        nc.vector.tensor_copy(
+            wb_codes[:].rearrange("p (t b u) -> p t b u", t=PACK, u=RUN), wb_w[:].rearrange("p (b t u) -> p t b u", t=PACK, u=RUN)
+        )
+        nc.vector.tensor_copy(
+            wb_sc[:].bitcast(I32).rearrange("p (t b u) -> p t b u", t=PACK, u=RUN // 4),
+            wb_s[:].bitcast(I32).rearrange("p (b t u) -> p t b u", t=PACK, u=RUN // 4),
+        )
 
         def bank_tile(b):
             return psum.tile([P, PACK, BANK_COLS], F32, name="bank%d" % b)
@@ -110,22 +118,9 @@ def tile_list_htabg_max_resP_kernel(
             nc.scalar.copy(yb_c[:], bank[:].rearrange("p t j -> p j t"))
             yb.append(yb_c)
 
-        picked01 = sb("picked01", [P, 2, J], F32)
-        for i in range(2):
-            nc.vector.tensor_tensor(picked01[:, i, :], x_planes[i][:].indirect(head_lists[:]), wgt[:], ALU.mult)
-        xg = [sb("xg%d" % g, [P, GROUP, PACK], BF16) for g in range(GROUPS)]
-        picked23 = [sb("picked23_%d" % g, [P, 2, GROUP], F32) for g in range(GROUPS)]
-
-        def pick(i, g):
-            offsets = head_lists[:, g * GROUP // PER_COL : (g + 1) * GROUP // PER_COL]
-            nc.vector.tensor_tensor(
-                picked23[g][:, i - 2, :], x_planes[i][:].indirect(offsets), wgt[:, g * GROUP : (g + 1) * GROUP], ALU.mult
-            )
-
-        for g in range(GROUPS):
-            nc.scalar.copy(xg[g][:, :, 0:2], picked01[:, :, g * GROUP : (g + 1) * GROUP].rearrange("p i j -> p j i"))
-        for g in range(GROUPS):
-            pick(2, g)
+        picked = sb("picked", [P, PACK, J], F32)
+        for i in range(PACK - 1):
+            nc.vector.tensor_tensor(picked[:, i, :], x_planes[i][:].indirect(head_lists[:]), wgt[:], ALU.mult)
 
         wa_bf = sb("wa_bf", [P, PACK, P, PACK], BF16)
         wd_bf = sb("wd_bf", [P, PACK, P, PACK], BF16)
@@ -135,71 +130,91 @@ def tile_list_htabg_max_resP_kernel(
         wd_sc = sb("wd_sc", [P, N], U8)
         out_codes = sb("out_codes", [P, J], U32)
         out_sc = sb("out_sc", [P, J], U8)
-
-        def deal(copy, dst, src):
-            copy(dst.rearrange("p t m i -> p m i t"), src.rearrange("p i (m t) -> p m i t", t=PACK))
-
+        xg = [sb("xg%d" % g, [P, GROUP, PACK], BF16) for g in range(GROUPS)]
+        xg_codes = [sb("xg_codes%d" % g, [P, GROUP], U32) for g in range(GROUPS)]
+        xg_sc = [sb("xg_sc%d" % g, [P, GROUP], U8) for g in range(GROUPS)]
+        h_bf = [sb("h_bf%d" % g, [P, GROUP, PACK], BF16) for g in range(GROUPS)]
+        h_codes = [sb("h_codes%d" % g, [P, GROUP], U32) for g in range(GROUPS)]
+        h_sc = [sb("h_sc%d" % g, [P, GROUP], U8) for g in range(GROUPS)]
+        out_sb = [sb("out%d" % g, [P, PACK, GROUP], F32) for g in range(GROUPS)]
+        out_bf = [sb("out_bf%d" % g, [P, GROUP, PACK], BF16) for g in range(GROUPS)]
         halves = GROUP // BANK_COLS
-        xg_q, h_q = {}, {}
 
-        def finish_picks(g):
-            pick(3, g)
-            nc.scalar.copy(xg[g][:, :, 2:4], picked23[g][:].rearrange("p i j -> p j i"))
-            xg_codes = sb("xg_codes%d" % g, [P, GROUP], U32)
-            xg_sc = sb("xg_sc%d" % g, [P, GROUP], U8)
-            quantize(xg_codes[:], xg_sc[:], xg[g][:].rearrange("p j i -> p (j i)"))
-            xg_q[g] = (xg_codes, xg_sc)
+        def weave(dst, src):
+            nc.scalar.copy(dst.rearrange("p (c q) i -> p c i q", q=4), src.rearrange("p i (c q) -> p c i q", q=4))
 
-        def first_layer(g):
-            xg_codes, xg_sc = xg_q[g]
-            h_bf = sb("h_bf%d" % g, [P, GROUP, PACK], BF16)
-            for u in range(halves):
-                cols = slice(u * BANK_COLS, (u + 1) * BANK_COLS)
-                bank = bank_tile(halves * (g % 2) + u)
-                project(bank, wa_codes, wa_sc, xg_codes[:, cols], xg_sc[:, cols])
-                nc.vector.tensor_tensor(h_bf[:, cols, :], bank[:].rearrange("p t j -> p j t"), yb[g * halves + u][:], ALU.max)
-            h_codes = sb("h_codes%d" % g, [P, GROUP], U32)
-            h_sc = sb("h_sc%d" % g, [P, GROUP], U8)
-            quantize(h_codes[:], h_sc[:], h_bf[:].rearrange("p j t -> p (j t)"))
-            h_q[g] = (h_codes, h_sc)
+        def flat(values):
+            return values[:].rearrange("p j i -> p (j i)")
 
-        def second_layer(g):
+        def last_pick(g):
             gcols = slice(g * GROUP, (g + 1) * GROUP)
-            h_codes, h_sc = h_q[g]
-            out_sb = sb("out%d" % g, [P, PACK, GROUP], F32)
-            out_bf = sb("out_bf%d" % g, [P, GROUP, PACK], BF16)
+            offsets = head_lists[:, g * GROUP // PER_COL : (g + 1) * GROUP // PER_COL]
+            nc.vector.tensor_tensor(picked[:, PACK - 1, gcols], x_planes[PACK - 1][:].indirect(offsets), wgt[:, gcols], ALU.mult)
+            weave(xg[g][:], picked[:, :, gcols])
+
+        def deal_wa(copy, h):
+            dst = wa_bf[:, :, h * (P // 2) : (h + 1) * (P // 2), :]
+            copy(dst.rearrange("p t (b u) i -> p b t i u", u=RUN), wa_raw[h][:].rearrange("p i (b t u) -> p b t i u", t=PACK, u=RUN))
+
+        def quantize_xg(g):
+            quantize(xg_codes[g][:], xg_sc[g][:], flat(xg[g]))
+
+        def join(g, first_bank):
             for u in range(halves):
                 cols = slice(u * BANK_COLS, (u + 1) * BANK_COLS)
-                bank = bank_tile(halves * g + u)
-                project(bank, wd_codes, wd_sc, h_codes[:, cols], h_sc[:, cols])
-                nc.vector.tensor_tensor(out_sb[:, :, cols], bank[:], res_sb[g][:, :, cols], ALU.add)
-                last = g == GROUPS - 1 and u == halves - 1
-                copy = nc.vector.tensor_copy if last else nc.scalar.copy
-                copy(
-                    out_bf[:, cols, :].rearrange("p (c q) t -> p c t q", q=4),
-                    out_sb[:, :, cols].rearrange("p t (c q) -> p c t q", q=4),
-                )
-            nc.sync.dma_start(out_rows[:, :, gcols], out_sb[:])
-            quantize(out_codes[:, gcols], out_sc[:, gcols], out_bf[:].rearrange("p j t -> p (j t)"))
+                bank = bank_tile(first_bank + u)
+                project(bank, wa_codes, wa_sc, xg_codes[g][:, cols], xg_sc[g][:, cols])
+                nc.vector.tensor_tensor(h_bf[g][:, cols, :], bank[:].rearrange("p t j -> p j t"), yb[g * halves + u][:], ALU.max)
+
+        def quantize_h(g):
+            quantize(h_codes[g][:], h_sc[g][:], flat(h_bf[g]))
+
+        def second_layer(g, u, first_bank):
+            cols = slice(u * BANK_COLS, (u + 1) * BANK_COLS)
+            bank = bank_tile(first_bank + u)
+            project(bank, wd_codes, wd_sc, h_codes[g][:, cols], h_sc[g][:, cols])
+            nc.vector.tensor_tensor(out_sb[g][:, :, cols], bank[:], res_sb[g][:, :, cols], ALU.add)
+            weave(out_bf[g][:, cols, :], out_sb[g][:, :, cols])
+            if u == halves - 1:
+                nc.sync.dma_start(out_rows[:, :, g * GROUP : (g + 1) * GROUP], out_sb[g][:])
+
+        def hand_on(g):
+            gcols = slice(g * GROUP, (g + 1) * GROUP)
+            quantize(out_codes[:, gcols], out_sc[:, gcols], flat(out_bf[g]))
             nc.sync.dma_start(words_of(out_1)[:, gcols], out_codes[:, gcols].bitcast(I32))
 
-        finish_picks(0)
-        deal(nc.scalar.copy, wa_bf[:, :, 0 : P // 2, :], wa_raw[0][:])
-        deal(nc.vector.tensor_copy, wa_bf[:, :, P // 2 : P, :], wa_raw[1][:])
+        last_pick(0)
+        deal_wa(nc.scalar.copy, 0)
+        for g in range(1, GROUPS):
+            last_pick(g)
+        deal_wa(nc.vector.tensor_copy, 1)
+        quantize_xg(0)
         quantize(wa_codes[:], wa_sc[:], wa_bf[:].rearrange("p t m i -> p (t m i)"))
-        finish_picks(1)
-        first_layer(0)
-        deal(nc.scalar.copy, wd_bf[:], wd_raw[:])
+        quantize_xg(1)
+        join(0, 0)
+        quantize_xg(2)
+        quantize_h(0)
+        join(1, 2)
+        quantize_xg(3)
+        quantize_h(1)
+        join(2, 4)
+        nc.scalar.copy(wd_bf[:].rearrange("p t m i -> p m i t"), wd_raw[:].rearrange("p i (m t) -> p m i t", t=PACK))
         quantize(wd_codes[:], wd_sc[:], wd_bf[:].rearrange("p t m i -> p (t m i)"))
-        finish_picks(2)
-        first_layer(1)
-        finish_picks(3)
-        second_layer(0)
-        first_layer(2)
-        second_layer(1)
-        first_layer(3)
-        second_layer(2)
-        second_layer(3)
+        quantize_h(2)
+        second_layer(0, 0, 6)
+        second_layer(0, 1, 6)
+        second_layer(1, 0, 2)
+        second_layer(1, 1, 2)
+        join(3, 6)
+        hand_on(0)
+        quantize_h(3)
+        second_layer(2, 0, 0)
+        hand_on(1)
+        second_layer(2, 1, 0)
+        second_layer(3, 0, 4)
+        second_layer(3, 1, 4)
+        hand_on(2)
+        hand_on(3)
         for q in range(4):
             queue = nc.sync if q % 2 == 0 else nc.scalar
             queue.dma_start(out_2[0, 4 * q : 4 * q + 4, :].bitcast(I32), out_sc[32 * q : 32 * q + 4, :].bitcast(I32))

@@ -31,8 +31,8 @@ def tile_list_htabg_max_resP_kernel(
         keep = ctx.enter_context(tc.tile_pool(name="keep", bufs=1))
         psum = ctx.enter_context(tc.psum_pool(name="psum", bufs=1))
 
-        def sb(name, shape, dtype):
-            return keep.tile(shape, dtype, name=name, align_bytes=64)
+        def sb(name, shape, dtype, tag=""):
+            return keep.tile(shape, dtype, name=name, align_bytes=64, tag=tag)
 
         def words_of(dram):
             return dram[0].rearrange("p c i -> p (c i)").bitcast(I32)
@@ -62,7 +62,7 @@ def tile_list_htabg_max_resP_kernel(
         wgt = sb("wgt", [P, J], F32)
         x_planes = [sb("x%d" % i, [P, T], F32) for i in range(PACK)]
         wa_raw = [sb("wa_raw%d" % h, [P, PACK, R // 2], F32) for h in range(2)]
-        wd_raw = sb("wd_raw", [P, PACK, N], F32)
+        wd_raw = sb("wd_raw", [P, PACK, N], F32, tag="staging")
         res_sb = [sb("res%d" % g, [P, PACK, GROUP], F32) for g in range(GROUPS)]
 
         nc.vector.memset(wb_s[:].bitcast(I32), 0)
@@ -77,12 +77,13 @@ def tile_list_htabg_max_resP_kernel(
             rows = tab_scales[0, 4 * q : 4 * q + 4, :].bitcast(I32)
             nc.sync.dma_start(tab_s[32 * q : 32 * q + 32, :].bitcast(I32), rows.partition_broadcast(8))
         nc.sync.dma_start(tab_w[:], words_of(tab_words))
-        nc.sync.dma_start(wb_w[:], words_of(wb_words))
         nc.sync.dma_start(head_lists[:], offs2)
+        nc.sync.dma_start(wgt[:], wgt2)
+        nc.sync.dma_start(x_planes[0][:], x_rows[:, 0, :])
+        nc.sync.dma_start(wb_w[:], words_of(wb_words))
         for q in range(4):
             nc.sync.dma_start(wb_s[32 * q : 32 * q + 4, :].bitcast(I32), wb_scales[0, 4 * q : 4 * q + 4, :].bitcast(I32))
-        nc.sync.dma_start(wgt[:], wgt2)
-        for i in range(PACK):
+        for i in range(1, PACK):
             nc.sync.dma_start(x_planes[i][:], x_rows[:, i, :])
         for h in range(2):
             nc.sync.dma_start(wa_raw[h][:], wa_rows[:, :, h * (R // 2) : (h + 1) * (R // 2)])
@@ -128,16 +129,14 @@ def tile_list_htabg_max_resP_kernel(
         wa_sc = sb("wa_sc", [P, R], U8)
         wd_codes = sb("wd_codes", [P, N], U32)
         wd_sc = sb("wd_sc", [P, N], U8)
-        out_codes = sb("out_codes", [P, J], U32)
         out_sc = sb("out_sc", [P, J], U8)
-        xg = [sb("xg%d" % g, [P, GROUP, PACK], BF16) for g in range(GROUPS)]
-        xg_codes = [sb("xg_codes%d" % g, [P, GROUP], U32) for g in range(GROUPS)]
-        xg_sc = [sb("xg_sc%d" % g, [P, GROUP], U8) for g in range(GROUPS)]
-        h_bf = [sb("h_bf%d" % g, [P, GROUP, PACK], BF16) for g in range(GROUPS)]
-        h_codes = [sb("h_codes%d" % g, [P, GROUP], U32) for g in range(GROUPS)]
-        h_sc = [sb("h_sc%d" % g, [P, GROUP], U8) for g in range(GROUPS)]
-        out_sb = [sb("out%d" % g, [P, PACK, GROUP], F32) for g in range(GROUPS)]
-        out_bf = [sb("out_bf%d" % g, [P, GROUP, PACK], BF16) for g in range(GROUPS)]
+        xg_codes = sb("xg_codes", [P, J], U32)
+        xg_sc = sb("xg_sc", [P, J], U8)
+        h_bf = [sb("h_bf%d" % k, [P, 2 * GROUP, PACK], BF16, tag="h_bf%d" % k) for k in range(2)]
+        h_codes = sb("h_codes", [P, J], U32)
+        h_sc = sb("h_sc", [P, J], U8)
+        out_sb = {g: sb("out%d" % g, [P, PACK, GROUP], F32) for g in (0, 2, 3)}
+        out_bf = sb("out_bf", [P, J, PACK], BF16)
         halves = GROUP // BANK_COLS
 
         def weave(dst, src):
@@ -146,75 +145,101 @@ def tile_list_htabg_max_resP_kernel(
         def flat(values):
             return values[:].rearrange("p j i -> p (j i)")
 
-        def last_pick(g):
-            gcols = slice(g * GROUP, (g + 1) * GROUP)
-            offsets = head_lists[:, g * GROUP // PER_COL : (g + 1) * GROUP // PER_COL]
+        def last_pick(start, stop):
+            gcols = slice(start, stop)
+            offsets = head_lists[:, start // PER_COL : stop // PER_COL]
             nc.vector.tensor_tensor(picked[:, PACK - 1, gcols], x_planes[PACK - 1][:].indirect(offsets), wgt[:, gcols], ALU.mult)
-            weave(xg[g][:], picked[:, :, gcols])
+
 
         def deal_wa(copy, h):
             dst = wa_bf[:, :, h * (P // 2) : (h + 1) * (P // 2), :]
             copy(dst.rearrange("p t (b u) i -> p b t i u", u=RUN), wa_raw[h][:].rearrange("p i (b t u) -> p b t i u", t=PACK, u=RUN))
 
-        def quantize_xg(g):
-            quantize(xg_codes[g][:], xg_sc[g][:], flat(xg[g]))
+        def weave_picks(name, start, stop, tag=""):
+            xg = sb(name, [P, stop - start, PACK], BF16, tag=tag)
+            weave(xg[:], picked[:, :, start:stop])
+            return xg
+
+        def quantize_xg(xg, start, stop):
+            quantize(xg_codes[:, start:stop], xg_sc[:, start:stop], flat(xg))
 
         def join(g, first_bank):
             for u in range(halves):
                 cols = slice(u * BANK_COLS, (u + 1) * BANK_COLS)
                 bank = bank_tile(first_bank + u)
-                project(bank, wa_codes, wa_sc, xg_codes[g][:, cols], xg_sc[g][:, cols])
-                nc.vector.tensor_tensor(h_bf[g][:, cols, :], bank[:].rearrange("p t j -> p j t"), yb[g * halves + u][:], ALU.max)
+                xcols = slice(g * GROUP + u * BANK_COLS, g * GROUP + (u + 1) * BANK_COLS)
+                project(bank, wa_codes, wa_sc, xg_codes[:, xcols], xg_sc[:, xcols])
+                hcols = slice((g % 2) * GROUP + u * BANK_COLS, (g % 2) * GROUP + (u + 1) * BANK_COLS)
+                nc.vector.tensor_tensor(h_bf[g // 2][:, hcols, :], bank[:].rearrange("p t j -> p j t"), yb[g * halves + u][:], ALU.max)
 
-        def quantize_h(g):
-            quantize(h_codes[g][:], h_sc[g][:], flat(h_bf[g]))
+        def quantize_h(k):
+            cols = slice(2 * k * GROUP, 2 * (k + 1) * GROUP)
+            quantize(h_codes[:, cols], h_sc[:, cols], flat(h_bf[k]))
+
+        def round_out(g, u):
+            start = g * GROUP + u * BANK_COLS
+            weave(out_bf[:, start : start + BANK_COLS, :], out_sb[g][:, :, u * BANK_COLS : (u + 1) * BANK_COLS])
 
         def second_layer(g, u, first_bank):
             cols = slice(u * BANK_COLS, (u + 1) * BANK_COLS)
             bank = bank_tile(first_bank + u)
-            project(bank, wd_codes, wd_sc, h_codes[g][:, cols], h_sc[g][:, cols])
-            nc.vector.tensor_tensor(out_sb[g][:, :, cols], bank[:], res_sb[g][:, :, cols], ALU.add)
-            weave(out_bf[g][:, cols, :], out_sb[g][:, :, cols])
-            if u == halves - 1:
+            jcols = slice(g * GROUP + u * BANK_COLS, g * GROUP + (u + 1) * BANK_COLS)
+            project(bank, wd_codes, wd_sc, h_codes[:, jcols], h_sc[:, jcols])
+            if g == 0:
+                nc.scalar.copy(y0[:, u], bank[:])
+                nc.gpsimd.tensor_tensor(out_sb[g][:, :, cols], y0[:, u], res_sb[g][:, :, cols], ALU.add)
+            else:
+                nc.vector.tensor_tensor(out_sb[g][:, :, cols], bank[:], res_sb[g][:, :, cols], ALU.add)
+            if g > 0:
+                round_out(g, u)
+            if g == GROUPS - 1:
+                start = g * GROUP + u * BANK_COLS
+                nc.sync.dma_start(out_rows[:, :, start : start + BANK_COLS], out_sb[g][:, :, cols])
+            elif u == halves - 1 and g > 0:
                 nc.sync.dma_start(out_rows[:, :, g * GROUP : (g + 1) * GROUP], out_sb[g][:])
 
-        def hand_on(g):
-            gcols = slice(g * GROUP, (g + 1) * GROUP)
-            quantize(out_codes[:, gcols], out_sc[:, gcols], flat(out_bf[g]))
-            nc.sync.dma_start(words_of(out_1)[:, gcols], out_codes[:, gcols].bitcast(I32))
+        def hand_on(start, stop):
+            cols = slice(start, stop)
+            quantize(out_codes[:, cols], out_sc[:, cols], out_bf[:, cols, :].rearrange("p j i -> p (j i)"))
+            nc.sync.dma_start(words_of(out_1)[:, cols], out_codes[:, cols].bitcast(I32))
 
-        last_pick(0)
+        last_pick(0, GROUP)
+        last_pick(GROUP, 2 * GROUP)
+        last_pick(2 * GROUP, J)
+        xg0 = weave_picks("xg0", 0, GROUP)
         deal_wa(nc.scalar.copy, 0)
-        for g in range(1, GROUPS):
-            last_pick(g)
-        deal_wa(nc.vector.tensor_copy, 1)
-        quantize_xg(0)
-        quantize(wa_codes[:], wa_sc[:], wa_bf[:].rearrange("p t m i -> p (t m i)"))
-        quantize_xg(1)
-        join(0, 0)
-        quantize_xg(2)
-        quantize_h(0)
-        join(1, 2)
-        quantize_xg(3)
-        quantize_h(1)
-        join(2, 4)
+        xg1 = weave_picks("xg1", GROUP, 2 * GROUP)
         nc.scalar.copy(wd_bf[:].rearrange("p t m i -> p m i t"), wd_raw[:].rearrange("p i (m t) -> p m i t", t=PACK))
+        xg2 = weave_picks("xg2", 2 * GROUP, J, tag="staging")
+        deal_wa(nc.vector.tensor_copy, 1)
+        quantize_xg(xg0, 0, GROUP)
+        quantize(wa_codes[:], wa_sc[:], wa_bf[:].rearrange("p t m i -> p (t m i)"))
+        quantize_xg(xg1, GROUP, 2 * GROUP)
+        join(0, 0)
+        join(1, 2)
         quantize(wd_codes[:], wd_sc[:], wd_bf[:].rearrange("p t m i -> p (t m i)"))
-        quantize_h(2)
-        second_layer(0, 0, 6)
-        second_layer(0, 1, 6)
-        second_layer(1, 0, 2)
-        second_layer(1, 1, 2)
-        join(3, 6)
-        hand_on(0)
-        quantize_h(3)
-        second_layer(2, 0, 0)
-        hand_on(1)
-        second_layer(2, 1, 0)
-        second_layer(3, 0, 4)
-        second_layer(3, 1, 4)
-        hand_on(2)
-        hand_on(3)
+        quantize_h(0)
+        quantize_xg(xg2, 2 * GROUP, J)
+        y0 = sb("y0", [P, halves, PACK, BANK_COLS], F32)
+        out_sb[1] = sb("out1", [P, PACK, GROUP], F32, tag="staging")
+        second_layer(0, 0, 4)
+        second_layer(0, 1, 4)
+        second_layer(1, 0, 6)
+        second_layer(1, 1, 6)
+        nc.sync.dma_start(out_rows[:, :, 0:GROUP], out_sb[0][:])
+        round_out(0, 0)
+        round_out(0, 1)
+        join(2, 0)
+        join(3, 2)
+        quantize_h(1)
+        out_codes = sb("out_codes", [P, J], U32, tag="h_bf1")
+        hand_on(0, 2 * GROUP)
+        second_layer(2, 0, 4)
+        second_layer(2, 1, 4)
+        second_layer(3, 0, 6)
+        second_layer(3, 1, 6)
+        hand_on(2 * GROUP, 3 * GROUP)
+        hand_on(3 * GROUP, J)
         for q in range(4):
             queue = nc.sync if q % 2 == 0 else nc.scalar
             queue.dma_start(out_2[0, 4 * q : 4 * q + 4, :].bitcast(I32), out_sc[32 * q : 32 * q + 4, :].bitcast(I32))

@@ -61,9 +61,9 @@ def tile_list_htabg_max_resP_kernel(
         wb_s = sb("wb_s", [P, R], U8)
         wgt = sb("wgt", [P, J], F32)
         x_planes = [sb("x%d" % i, [P, T], F32) for i in range(PACK)]
-        wa_raw = [sb("wa_raw%d" % h, [P, PACK, R // 2], F32) for h in range(2)]
+        wa_raw = sb("wa_raw", [P, PACK, R], F32, tag="wa_raw")
         wd_raw = sb("wd_raw", [P, PACK, N], F32, tag="staging")
-        res_sb = [sb("res%d" % g, [P, PACK, GROUP], F32) for g in range(GROUPS)]
+        res_sb = [sb("res%d" % k, [P, PACK, J // 2], F32, tag="res%d" % k) for k in range(2)]
 
         nc.vector.memset(wb_s[:].bitcast(I32), 0)
 
@@ -85,13 +85,12 @@ def tile_list_htabg_max_resP_kernel(
             nc.sync.dma_start(wb_s[32 * q : 32 * q + 4, :].bitcast(I32), wb_scales[0, 4 * q : 4 * q + 4, :].bitcast(I32))
         for i in range(1, PACK):
             nc.sync.dma_start(x_planes[i][:], x_rows[:, i, :])
-        for h in range(2):
-            nc.sync.dma_start(wa_raw[h][:], wa_rows[:, :, h * (R // 2) : (h + 1) * (R // 2)])
+        nc.sync.dma_start(wa_raw[:], wa_rows)
         wd_rows = wd.rearrange("(b t u) n -> t b u n", t=PACK, u=RUN)
         for t in range(PACK):
             nc.sync.dma_start(wd_raw[:, t, :], wd_rows[t])
-        for g in range(GROUPS):
-            nc.sync.dma_start(res_sb[g][:], res_rows[:, :, g * GROUP : (g + 1) * GROUP])
+        for k in range(2):
+            nc.sync.dma_start(res_sb[k][:], res_rows[:, :, k * (J // 2) : (k + 1) * (J // 2)])
 
         v_codes = sb("v_codes", [P, J], U32)
         v_scales = sb("v_scales", [P, J], U8)
@@ -129,15 +128,20 @@ def tile_list_htabg_max_resP_kernel(
         wa_sc = sb("wa_sc", [P, R], U8)
         wd_codes = sb("wd_codes", [P, N], U32)
         wd_sc = sb("wd_sc", [P, N], U8)
+        out_codes = sb("out_codes", [P, J], U32)
         out_sc = sb("out_sc", [P, J], U8)
-        xg_codes = sb("xg_codes", [P, J], U32)
+        xg_codes = [sb("xg_codes0", [P, J // 2], U32)]
         xg_sc = sb("xg_sc", [P, J], U8)
-        h_bf = [sb("h_bf%d" % k, [P, 2 * GROUP, PACK], BF16, tag="h_bf%d" % k) for k in range(2)]
-        h_codes = sb("h_codes", [P, J], U32)
-        h_sc = sb("h_sc", [P, J], U8)
-        out_sb = {g: sb("out%d" % g, [P, PACK, GROUP], F32) for g in (0, 2, 3)}
-        out_bf = sb("out_bf", [P, J, PACK], BF16)
+        h_bf = [sb("h_bf%d" % g, [P, GROUP, PACK], BF16, tag="h_bf%d" % g) for g in range(GROUPS)]
+        h_codes = [sb("h_codes%d" % g, [P, GROUP], U32) for g in range(GROUPS)]
+        h_sc = [sb("h_sc%d" % g, [P, GROUP], U8) for g in range(GROUPS)]
+        out_sb = [sb("out%d" % g, [P, PACK, GROUP], F32) for g in range(GROUPS)]
+        out_bf = [sb("out_bf%d" % g, [P, GROUP, PACK], BF16) for g in range(GROUPS)]
         halves = GROUP // BANK_COLS
+
+        def half_cols(g, u):
+            start = (g % 2) * GROUP + u * BANK_COLS
+            return slice(start, start + BANK_COLS)
 
         def weave(dst, src):
             nc.scalar.copy(dst.rearrange("p (c q) i -> p c i q", q=4), src.rearrange("p i (c q) -> p c i q", q=4))
@@ -153,7 +157,7 @@ def tile_list_htabg_max_resP_kernel(
 
         def deal_wa(copy, h):
             dst = wa_bf[:, :, h * (P // 2) : (h + 1) * (P // 2), :]
-            copy(dst.rearrange("p t (b u) i -> p b t i u", u=RUN), wa_raw[h][:].rearrange("p i (b t u) -> p b t i u", t=PACK, u=RUN))
+            copy(dst.rearrange("p t (b u) i -> p b t i u", u=RUN), wa_raw[:, :, h * (R // 2) : (h + 1) * (R // 2)].rearrange("p i (b t u) -> p b t i u", t=PACK, u=RUN))
 
         def weave_picks(name, start, stop, tag=""):
             xg = sb(name, [P, stop - start, PACK], BF16, tag=tag)
@@ -161,85 +165,75 @@ def tile_list_htabg_max_resP_kernel(
             return xg
 
         def quantize_xg(xg, start, stop):
-            quantize(xg_codes[:, start:stop], xg_sc[:, start:stop], flat(xg))
+            quantize(xg_codes[start // (J // 2)][:, start % (J // 2) : (stop - 1) % (J // 2) + 1], xg_sc[:, start:stop], flat(xg))
 
-        def join(g, first_bank):
-            for u in range(halves):
+        def join(g, u, first_bank):
+            if True:
                 cols = slice(u * BANK_COLS, (u + 1) * BANK_COLS)
                 bank = bank_tile(first_bank + u)
                 xcols = slice(g * GROUP + u * BANK_COLS, g * GROUP + (u + 1) * BANK_COLS)
-                project(bank, wa_codes, wa_sc, xg_codes[:, xcols], xg_sc[:, xcols])
-                hcols = slice((g % 2) * GROUP + u * BANK_COLS, (g % 2) * GROUP + (u + 1) * BANK_COLS)
-                nc.vector.tensor_tensor(h_bf[g // 2][:, hcols, :], bank[:].rearrange("p t j -> p j t"), yb[g * halves + u][:], ALU.max)
+                project(bank, wa_codes, wa_sc, xg_codes[g // 2][:, half_cols(g, u)], xg_sc[:, xcols])
+                nc.vector.tensor_tensor(h_bf[g][:, cols, :], bank[:].rearrange("p t j -> p j t"), yb[g * halves + u][:], ALU.max)
 
-        def quantize_h(k):
-            cols = slice(2 * k * GROUP, 2 * (k + 1) * GROUP)
-            quantize(h_codes[:, cols], h_sc[:, cols], flat(h_bf[k]))
-
-        def round_out(g, u):
-            start = g * GROUP + u * BANK_COLS
-            weave(out_bf[:, start : start + BANK_COLS, :], out_sb[g][:, :, u * BANK_COLS : (u + 1) * BANK_COLS])
+        def quantize_h(g):
+            quantize(h_codes[g][:], h_sc[g][:], flat(h_bf[g]))
 
         def second_layer(g, u, first_bank):
             cols = slice(u * BANK_COLS, (u + 1) * BANK_COLS)
             bank = bank_tile(first_bank + u)
-            jcols = slice(g * GROUP + u * BANK_COLS, g * GROUP + (u + 1) * BANK_COLS)
-            project(bank, wd_codes, wd_sc, h_codes[:, jcols], h_sc[:, jcols])
-            if g == 0:
-                nc.scalar.copy(y0[:, u], bank[:])
-                nc.gpsimd.tensor_tensor(out_sb[g][:, :, cols], y0[:, u], res_sb[g][:, :, cols], ALU.add)
-            else:
-                nc.vector.tensor_tensor(out_sb[g][:, :, cols], bank[:], res_sb[g][:, :, cols], ALU.add)
-            if g > 0:
-                round_out(g, u)
+            project(bank, wd_codes, wd_sc, h_codes[g][:, cols], h_sc[g][:, cols])
+            nc.vector.tensor_tensor(out_sb[g][:, :, cols], bank[:], res_sb[g // 2][:, :, half_cols(g, u)], ALU.add)
+            weave(out_bf[g][:, cols, :], out_sb[g][:, :, cols])
             if g == GROUPS - 1:
                 start = g * GROUP + u * BANK_COLS
                 nc.sync.dma_start(out_rows[:, :, start : start + BANK_COLS], out_sb[g][:, :, cols])
-            elif u == halves - 1 and g > 0:
+            elif u == halves - 1:
                 nc.sync.dma_start(out_rows[:, :, g * GROUP : (g + 1) * GROUP], out_sb[g][:])
 
-        def hand_on(start, stop):
-            cols = slice(start, stop)
-            quantize(out_codes[:, cols], out_sc[:, cols], out_bf[:, cols, :].rearrange("p j i -> p (j i)"))
-            nc.sync.dma_start(words_of(out_1)[:, cols], out_codes[:, cols].bitcast(I32))
+        def hand_on(g):
+            gcols = slice(g * GROUP, (g + 1) * GROUP)
+            quantize(out_codes[:, gcols], out_sc[:, gcols], flat(out_bf[g]))
+            nc.sync.dma_start(words_of(out_1)[:, gcols], out_codes[:, gcols].bitcast(I32))
 
         last_pick(0, GROUP)
         last_pick(GROUP, 2 * GROUP)
         last_pick(2 * GROUP, J)
         xg0 = weave_picks("xg0", 0, GROUP)
         deal_wa(nc.scalar.copy, 0)
-        xg1 = weave_picks("xg1", GROUP, 2 * GROUP)
+        deal_wa(nc.vector.tensor_copy, 1)
+        xg1 = weave_picks("xg1", GROUP, 2 * GROUP, tag="wa_raw")
         nc.scalar.copy(wd_bf[:].rearrange("p t m i -> p m i t"), wd_raw[:].rearrange("p i (m t) -> p m i t", t=PACK))
         xg2 = weave_picks("xg2", 2 * GROUP, J, tag="staging")
-        deal_wa(nc.vector.tensor_copy, 1)
         quantize_xg(xg0, 0, GROUP)
         quantize(wa_codes[:], wa_sc[:], wa_bf[:].rearrange("p t m i -> p (t m i)"))
         quantize_xg(xg1, GROUP, 2 * GROUP)
-        join(0, 0)
-        join(1, 2)
+        join(0, 0, 0)
+        join(0, 1, 0)
+        join(1, 0, 2)
         quantize(wd_codes[:], wd_sc[:], wd_bf[:].rearrange("p t m i -> p (t m i)"))
         quantize_h(0)
-        quantize_xg(xg2, 2 * GROUP, J)
-        y0 = sb("y0", [P, halves, PACK, BANK_COLS], F32)
-        out_sb[1] = sb("out1", [P, PACK, GROUP], F32, tag="staging")
+        join(1, 1, 2)
         second_layer(0, 0, 4)
+        quantize_h(1)
         second_layer(0, 1, 4)
         second_layer(1, 0, 6)
+        xg_codes.append(sb("xg_codes1", [P, J // 2], U32, tag="h_bf1"))
+        quantize_xg(xg2, 2 * GROUP, J)
         second_layer(1, 1, 6)
-        nc.sync.dma_start(out_rows[:, :, 0:GROUP], out_sb[0][:])
-        round_out(0, 0)
-        round_out(0, 1)
-        join(2, 0)
-        join(3, 2)
-        quantize_h(1)
-        out_codes = sb("out_codes", [P, J], U32, tag="h_bf1")
-        hand_on(0, 2 * GROUP)
+        hand_on(0)
+        join(2, 0, 0)
+        join(2, 1, 0)
+        join(3, 0, 2)
+        quantize_h(2)
+        join(3, 1, 2)
+        hand_on(1)
+        quantize_h(3)
         second_layer(2, 0, 4)
         second_layer(2, 1, 4)
         second_layer(3, 0, 6)
         second_layer(3, 1, 6)
-        hand_on(2 * GROUP, 3 * GROUP)
-        hand_on(3 * GROUP, J)
+        hand_on(2)
+        hand_on(3)
         for q in range(4):
             queue = nc.sync if q % 2 == 0 else nc.scalar
             queue.dma_start(out_2[0, 4 * q : 4 * q + 4, :].bitcast(I32), out_sc[32 * q : 32 * q + 4, :].bitcast(I32))

@@ -16,11 +16,12 @@ ALU = mybir.AluOpType
 
 P = 128
 PACK = 4
-BANK_COLS = 128
-GROUP = 256
-GROUPS = J // GROUP
+QUADRANTS, QUADRANT = 4, 32
 RUN = 8
 PER_COL = 16
+BANK_COLS = 128
+GROUP = 2 * BANK_COLS
+GROUPS = J // GROUP
 
 
 def tile_list_htabg_max_resP_kernel(
@@ -34,24 +35,42 @@ def tile_list_htabg_max_resP_kernel(
         def sb(name, shape, dtype, tag=""):
             return keep.tile(shape, dtype, name=name, align_bytes=64, tag=tag)
 
+        def bank_tile(bank):
+            return psum.tile([P, PACK, BANK_COLS], F32, name="bank%d" % bank)
+
         def words_of(dram):
             return dram[0].rearrange("p c i -> p (c i)").bitcast(I32)
+
+        def scale_rows(dram, q):
+            return dram[0, PACK * q : PACK * (q + 1), :].bitcast(I32)
+
+        def live_rows(scales, q):
+            return scales[QUADRANT * q : QUADRANT * q + PACK, :].bitcast(I32)
+
+        def group_cols(g):
+            return slice(g * GROUP, (g + 1) * GROUP)
+
+        def half_cols(g, half):
+            return slice(g * GROUP + half * BANK_COLS, g * GROUP + (half + 1) * BANK_COLS)
 
         def quantize(codes, scales, values):
             nc.vector.quantize_mx(out=codes.bitcast(FP8X4), scales=scales, in_=values)
 
         def project(bank, w_codes, w_scales, codes, scales):
             for t in range(PACK):
-                cols = slice(t * P, (t + 1) * P)
+                w_cols = slice(t * P, (t + 1) * P)
                 nc.tensor.matmul_mx(
                     out=bank[:, t, :],
-                    lhsT=w_codes[:, cols].bitcast(FP8X4),
-                    lhsT_scale=w_scales[:, cols],
+                    lhsT=w_codes[:, w_cols].bitcast(FP8X4),
+                    lhsT_scale=w_scales[:, w_cols],
                     rhs=codes.bitcast(FP8X4),
                     rhs_scale=scales,
                     start=True,
                     stop=True,
                 )
+
+        def weave(dst, src):
+            nc.scalar.copy(dst.rearrange("p (c e) i -> p c i e", e=2), src.rearrange("p i (c e) -> p c i e", e=2))
 
         tab_list = keep.tile([P, J // PER_COL], U16, name="tab_list")
         head_lists = keep.tile([P, J // PER_COL], U16, name="head_lists")
@@ -61,36 +80,34 @@ def tile_list_htabg_max_resP_kernel(
         wb_s = sb("wb_s", [P, R], U8)
         wgt = sb("wgt", [P, J], F32)
         x_planes = [sb("x%d" % i, [P, T], F32) for i in range(PACK)]
-        wa_raw = sb("wa_raw", [P, PACK, R], F32, tag="wa_raw")
-        wd_raw = sb("wd_raw", [P, PACK, N], F32, tag="staging")
-        res_sb = [sb("res%d" % k, [P, PACK, J // 2], F32, tag="res%d" % k) for k in range(2)]
+        wa_raw = sb("wa_raw", [P, PACK, R], F32, tag="wa_buffer")
+        wd_raw = sb("wd_raw", [P, PACK, N], F32, tag="wd_buffer")
+        res_sb = [sb("res%d" % side, [P, PACK, J // 2], F32) for side in range(2)]
 
         nc.vector.memset(wb_s[:].bitcast(I32), 0)
 
         x_rows = xT.rearrange("(p i) t -> p i t", i=PACK)
-        wa_rows = wa.rearrange("(p i) r -> p i r", i=PACK)
+        wd_rows = wd.rearrange("(b t u) n -> t b u n", t=PACK, u=RUN)
         res_rows = res.rearrange("(p t) j -> p t j", t=PACK)
         out_rows = out_0.rearrange("(p t) j -> p t j", t=PACK)
 
         nc.sync.dma_start(tab_list[:], offs)
-        for q in range(4):
-            rows = tab_scales[0, 4 * q : 4 * q + 4, :].bitcast(I32)
-            nc.sync.dma_start(tab_s[32 * q : 32 * q + 32, :].bitcast(I32), rows.partition_broadcast(8))
+        for q in range(QUADRANTS):
+            quadrant = tab_s[QUADRANT * q : QUADRANT * (q + 1), :].bitcast(I32)
+            nc.sync.dma_start(quadrant, scale_rows(tab_scales, q).partition_broadcast(QUADRANT // PACK))
         nc.sync.dma_start(tab_w[:], words_of(tab_words))
-        nc.sync.dma_start(head_lists[:], offs2)
-        nc.sync.dma_start(wgt[:], wgt2)
-        nc.sync.dma_start(x_planes[0][:], x_rows[:, 0, :])
         nc.sync.dma_start(wb_w[:], words_of(wb_words))
-        for q in range(4):
-            nc.sync.dma_start(wb_s[32 * q : 32 * q + 4, :].bitcast(I32), wb_scales[0, 4 * q : 4 * q + 4, :].bitcast(I32))
-        for i in range(1, PACK):
+        nc.sync.dma_start(head_lists[:], offs2)
+        for q in range(QUADRANTS):
+            nc.sync.dma_start(live_rows(wb_s, q), scale_rows(wb_scales, q))
+        nc.sync.dma_start(wgt[:], wgt2)
+        for i in range(PACK):
             nc.sync.dma_start(x_planes[i][:], x_rows[:, i, :])
-        nc.sync.dma_start(wa_raw[:], wa_rows)
-        wd_rows = wd.rearrange("(b t u) n -> t b u n", t=PACK, u=RUN)
+        nc.sync.dma_start(wa_raw[:], wa.rearrange("(p i) r -> p i r", i=PACK))
         for t in range(PACK):
             nc.sync.dma_start(wd_raw[:, t, :], wd_rows[t])
-        for k in range(2):
-            nc.sync.dma_start(res_sb[k][:], res_rows[:, :, k * (J // 2) : (k + 1) * (J // 2)])
+        for side in range(2):
+            nc.sync.dma_start(res_sb[side][:], res_rows[:, :, side * (J // 2) : (side + 1) * (J // 2)])
 
         v_codes = sb("v_codes", [P, J], U32)
         v_scales = sb("v_scales", [P, J], U8)
@@ -99,16 +116,13 @@ def tile_list_htabg_max_resP_kernel(
         nc.vector.tensor_copy(v_scales[:], tab_s[:].indirect(tab_list[:]))
         nc.vector.tensor_copy(v_codes[:], tab_w[:].bitcast(U32).indirect(tab_list[:]))
         nc.vector.tensor_copy(
-            wb_codes[:].rearrange("p (t b u) -> p t b u", t=PACK, u=RUN), wb_w[:].rearrange("p (b t u) -> p t b u", t=PACK, u=RUN)
+            wb_codes[:].rearrange("p (t b u) -> p t b u", t=PACK, u=RUN),
+            wb_w[:].rearrange("p (b t u) -> p t b u", t=PACK, u=RUN),
         )
         nc.vector.tensor_copy(
             wb_sc[:].bitcast(I32).rearrange("p (t b u) -> p t b u", t=PACK, u=RUN // 4),
             wb_s[:].bitcast(I32).rearrange("p (b t u) -> p t b u", t=PACK, u=RUN // 4),
         )
-
-        def bank_tile(b):
-            return psum.tile([P, PACK, BANK_COLS], F32, name="bank%d" % b)
-
         yb = []
         for c in range(J // BANK_COLS):
             cols = slice(c * BANK_COLS, (c + 1) * BANK_COLS)
@@ -130,110 +144,96 @@ def tile_list_htabg_max_resP_kernel(
         wd_sc = sb("wd_sc", [P, N], U8)
         out_codes = sb("out_codes", [P, J], U32)
         out_sc = sb("out_sc", [P, J], U8)
-        xg_codes = [sb("xg_codes0", [P, J // 2], U32)]
+        xg_codes = sb("xg_codes", [P, J], U32)
         xg_sc = sb("xg_sc", [P, J], U8)
-        h_bf = [sb("h_bf%d" % g, [P, GROUP, PACK], BF16, tag="h_bf%d" % g) for g in range(GROUPS)]
+        h_bf = [sb("h_bf%d" % g, [P, GROUP, PACK], BF16) for g in range(GROUPS)]
         h_codes = [sb("h_codes%d" % g, [P, GROUP], U32) for g in range(GROUPS)]
         h_sc = [sb("h_sc%d" % g, [P, GROUP], U8) for g in range(GROUPS)]
         out_sb = [sb("out%d" % g, [P, PACK, GROUP], F32) for g in range(GROUPS)]
         out_bf = [sb("out_bf%d" % g, [P, GROUP, PACK], BF16) for g in range(GROUPS)]
-        halves = GROUP // BANK_COLS
 
-        def half_cols(g, u):
-            start = (g % 2) * GROUP + u * BANK_COLS
-            return slice(start, start + BANK_COLS)
+        for start, stop in ((0, GROUP), (GROUP, 2 * GROUP), (2 * GROUP, J)):
+            window = x_planes[PACK - 1][:].indirect(head_lists[:, start // PER_COL : stop // PER_COL])
+            nc.vector.tensor_tensor(picked[:, PACK - 1, start:stop], window, wgt[:, start:stop], ALU.mult)
 
-        def weave(dst, src):
-            nc.scalar.copy(dst.rearrange("p (c q) i -> p c i q", q=4), src.rearrange("p i (c q) -> p c i q", q=4))
+        xg0 = sb("xg0", [P, GROUP, PACK], BF16)
+        weave(xg0[:], picked[:, :, group_cols(0)])
+        wa_dealt = wa_raw[:].rearrange("p i (b t c e) -> p t b c i e", t=PACK, c=RUN // 2, e=2)
+        for t in range(PACK):
+            copy = nc.scalar.copy if t < PACK // 2 else nc.vector.tensor_copy
+            copy(wa_bf[:, t].rearrange("p (b c e) i -> p b c i e", c=RUN // 2, e=2), wa_dealt[:, t])
+        xg12 = sb("xg12", [P, 2, GROUP, PACK], BF16, tag="wa_buffer")
+        weave(xg12[:, 0], picked[:, :, group_cols(1)])
+        weave(xg12[:, 1], picked[:, :, group_cols(2)])
+        nc.scalar.copy(
+            wd_bf[:].rearrange("p (s e) m i -> p s m e i", e=2),
+            wd_raw[:].rearrange("p i (m s e) -> p s m e i", s=2, e=2),
+        )
+        xg3 = sb("xg3", [P, GROUP, PACK], BF16, tag="wd_buffer")
+        weave(xg3[:], picked[:, :, group_cols(3)])
+        xg = [xg0[:], xg12[:, 0], xg12[:, 1], xg3[:]]
 
-        def flat(values):
-            return values[:].rearrange("p j i -> p (j i)")
+        def quantize_xg(g):
+            quantize(xg_codes[:, group_cols(g)], xg_sc[:, group_cols(g)], xg[g].rearrange("p j i -> p (j i)"))
 
-        def last_pick(start, stop):
-            gcols = slice(start, stop)
-            offsets = head_lists[:, start // PER_COL : stop // PER_COL]
-            nc.vector.tensor_tensor(picked[:, PACK - 1, gcols], x_planes[PACK - 1][:].indirect(offsets), wgt[:, gcols], ALU.mult)
-
-
-        def deal_wa(copy, h):
-            dst = wa_bf[:, :, h * (P // 2) : (h + 1) * (P // 2), :]
-            copy(dst.rearrange("p t (b u) i -> p b t i u", u=RUN), wa_raw[:, :, h * (R // 2) : (h + 1) * (R // 2)].rearrange("p i (b t u) -> p b t i u", t=PACK, u=RUN))
-
-        def weave_picks(name, start, stop, tag=""):
-            xg = sb(name, [P, stop - start, PACK], BF16, tag=tag)
-            weave(xg[:], picked[:, :, start:stop])
-            return xg
-
-        def quantize_xg(xg, start, stop):
-            quantize(xg_codes[start // (J // 2)][:, start % (J // 2) : (stop - 1) % (J // 2) + 1], xg_sc[:, start:stop], flat(xg))
-
-        def join(g, u, first_bank):
-            if True:
-                cols = slice(u * BANK_COLS, (u + 1) * BANK_COLS)
-                bank = bank_tile(first_bank + u)
-                xcols = slice(g * GROUP + u * BANK_COLS, g * GROUP + (u + 1) * BANK_COLS)
-                project(bank, wa_codes, wa_sc, xg_codes[g // 2][:, half_cols(g, u)], xg_sc[:, xcols])
-                nc.vector.tensor_tensor(h_bf[g][:, cols, :], bank[:].rearrange("p t j -> p j t"), yb[g * halves + u][:], ALU.max)
+        def join(g, half, first_bank):
+            cols = half_cols(g, half)
+            bank = bank_tile(first_bank + half)
+            project(bank, wa_codes, wa_sc, xg_codes[:, cols], xg_sc[:, cols])
+            ya = bank[:].rearrange("p t j -> p j t")
+            nc.vector.tensor_tensor(h_bf[g][:, half_cols(0, half), :], ya, yb[2 * g + half][:], ALU.max)
 
         def quantize_h(g):
-            quantize(h_codes[g][:], h_sc[g][:], flat(h_bf[g]))
+            quantize(h_codes[g][:], h_sc[g][:], h_bf[g][:].rearrange("p j t -> p (j t)"))
 
-        def second_layer(g, u, first_bank):
-            cols = slice(u * BANK_COLS, (u + 1) * BANK_COLS)
-            bank = bank_tile(first_bank + u)
-            project(bank, wd_codes, wd_sc, h_codes[g][:, cols], h_sc[g][:, cols])
-            nc.vector.tensor_tensor(out_sb[g][:, :, cols], bank[:], res_sb[g // 2][:, :, half_cols(g, u)], ALU.add)
-            weave(out_bf[g][:, cols, :], out_sb[g][:, :, cols])
+        def second_layer(g, half, first_bank):
+            local = half_cols(0, half)
+            bank = bank_tile(first_bank + half)
+            project(bank, wd_codes, wd_sc, h_codes[g][:, local], h_sc[g][:, local])
+            residual = res_sb[g // 2][:, :, half_cols(g % 2, half)]
+            nc.vector.tensor_tensor(out_sb[g][:, :, local], bank[:], residual, ALU.add)
+            weave(out_bf[g][:, local, :], out_sb[g][:, :, local])
             if g == GROUPS - 1:
-                start = g * GROUP + u * BANK_COLS
-                nc.sync.dma_start(out_rows[:, :, start : start + BANK_COLS], out_sb[g][:, :, cols])
-            elif u == halves - 1:
-                nc.sync.dma_start(out_rows[:, :, g * GROUP : (g + 1) * GROUP], out_sb[g][:])
+                nc.sync.dma_start(out_rows[:, :, half_cols(g, half)], out_sb[g][:, :, local])
+            elif half == 1:
+                nc.sync.dma_start(out_rows[:, :, group_cols(g)], out_sb[g][:])
 
         def hand_on(g):
-            gcols = slice(g * GROUP, (g + 1) * GROUP)
-            quantize(out_codes[:, gcols], out_sc[:, gcols], flat(out_bf[g]))
-            nc.sync.dma_start(words_of(out_1)[:, gcols], out_codes[:, gcols].bitcast(I32))
+            cols = group_cols(g)
+            quantize(out_codes[:, cols], out_sc[:, cols], out_bf[g][:].rearrange("p j t -> p (j t)"))
+            nc.sync.dma_start(words_of(out_1)[:, cols], out_codes[:, cols].bitcast(I32))
 
-        last_pick(0, GROUP)
-        last_pick(GROUP, 2 * GROUP)
-        last_pick(2 * GROUP, J)
-        xg0 = weave_picks("xg0", 0, GROUP)
-        deal_wa(nc.scalar.copy, 0)
-        deal_wa(nc.vector.tensor_copy, 1)
-        xg1 = weave_picks("xg1", GROUP, 2 * GROUP, tag="wa_raw")
-        nc.scalar.copy(wd_bf[:].rearrange("p t m i -> p m i t"), wd_raw[:].rearrange("p i (m t) -> p m i t", t=PACK))
-        xg2 = weave_picks("xg2", 2 * GROUP, J, tag="staging")
-        quantize_xg(xg0, 0, GROUP)
+        quantize_xg(0)
         quantize(wa_codes[:], wa_sc[:], wa_bf[:].rearrange("p t m i -> p (t m i)"))
-        quantize_xg(xg1, GROUP, 2 * GROUP)
+        quantize_xg(1)
         join(0, 0, 0)
         join(0, 1, 0)
         join(1, 0, 2)
-        quantize(wd_codes[:], wd_sc[:], wd_bf[:].rearrange("p t m i -> p (t m i)"))
         quantize_h(0)
         join(1, 1, 2)
-        second_layer(0, 0, 4)
+        quantize_xg(2)
         quantize_h(1)
-        second_layer(0, 1, 4)
-        second_layer(1, 0, 6)
-        xg_codes.append(sb("xg_codes1", [P, J // 2], U32, tag="h_bf1"))
-        quantize_xg(xg2, 2 * GROUP, J)
-        second_layer(1, 1, 6)
-        hand_on(0)
+        quantize(wd_codes[:], wd_sc[:], wd_bf[:].rearrange("p t m i -> p (t m i)"))
         join(2, 0, 0)
         join(2, 1, 0)
-        join(3, 0, 2)
+        second_layer(0, 0, 4)
         quantize_h(2)
-        join(3, 1, 2)
+        second_layer(0, 1, 4)
+        quantize_xg(3)
+        second_layer(1, 0, 6)
+        second_layer(1, 1, 6)
+        hand_on(0)
+        join(3, 0, 4)
+        join(3, 1, 4)
         hand_on(1)
         quantize_h(3)
-        second_layer(2, 0, 4)
-        second_layer(2, 1, 4)
-        second_layer(3, 0, 6)
-        second_layer(3, 1, 6)
+        second_layer(2, 0, 0)
+        second_layer(2, 1, 0)
+        second_layer(3, 0, 2)
+        second_layer(3, 1, 2)
         hand_on(2)
         hand_on(3)
-        for q in range(4):
+
+        for q in range(QUADRANTS):
             queue = nc.sync if q % 2 == 0 else nc.scalar
-            queue.dma_start(out_2[0, 4 * q : 4 * q + 4, :].bitcast(I32), out_sc[32 * q : 32 * q + 4, :].bitcast(I32))
+            queue.dma_start(scale_rows(out_2, q), live_rows(out_sc, q))

from contextlib import ExitStack

import concourse.mybir as mybir

K, L, R, N, T, J = 512, 512, 512, 512, 2048, 1024
FLOPS = 2 * J * (K * R + L * R + R * N)

F32 = mybir.dt.float32
BF16 = mybir.dt.bfloat16
I32 = mybir.dt.int32
U32 = mybir.dt.uint32
U16 = mybir.dt.uint16
U8 = mybir.dt.uint8
FP8X4 = mybir.dt.float8_e4m3fn_x4
ALU = mybir.AluOpType

P = 128
PACK = 4
QUADRANTS, QUADRANT = 4, 32
RUN = 8
PER_COL = 16
BANK_COLS = 128
GROUP = 2 * BANK_COLS
GROUPS = J // GROUP


def tile_list_htabg_max_resP_kernel(
    tc, tab_words, tab_scales, xT, wgt2, wa, wb_words, wb_scales, wd, res, offs, offs2, out_0, out_1, out_2
):
    nc = tc.nc
    with ExitStack() as ctx:
        keep = ctx.enter_context(tc.tile_pool(name="keep", bufs=1))
        psum = ctx.enter_context(tc.psum_pool(name="psum", bufs=1))

        def sb(name, shape, dtype, tag=""):
            return keep.tile(shape, dtype, name=name, align_bytes=64, tag=tag)

        def bank_tile(bank):
            return psum.tile([P, PACK, BANK_COLS], F32, name="bank%d" % bank)

        def words_of(dram):
            return dram[0].rearrange("p c i -> p (c i)").bitcast(I32)

        def scale_rows(dram, q):
            return dram[0, PACK * q : PACK * (q + 1), :].bitcast(I32)

        def live_rows(scales, q):
            return scales[QUADRANT * q : QUADRANT * q + PACK, :].bitcast(I32)

        def group_cols(g):
            return slice(g * GROUP, (g + 1) * GROUP)

        def half_cols(g, half):
            return slice(g * GROUP + half * BANK_COLS, g * GROUP + (half + 1) * BANK_COLS)

        def quantize(codes, scales, values):
            nc.vector.quantize_mx(out=codes.bitcast(FP8X4), scales=scales, in_=values)

        def project(bank, w_codes, w_scales, codes, scales):
            for t in range(PACK):
                w_cols = slice(t * P, (t + 1) * P)
                nc.tensor.matmul_mx(
                    out=bank[:, t, :],
                    lhsT=w_codes[:, w_cols].bitcast(FP8X4),
                    lhsT_scale=w_scales[:, w_cols],
                    rhs=codes.bitcast(FP8X4),
                    rhs_scale=scales,
                    start=True,
                    stop=True,
                )

        def weave(dst, src):
            nc.scalar.copy(dst.rearrange("p (c e) i -> p c i e", e=2), src.rearrange("p i (c e) -> p c i e", e=2))

        tab_list = keep.tile([P, J // PER_COL], U16, name="tab_list")
        head_lists = keep.tile([P, J // PER_COL], U16, name="head_lists")
        tab_w = sb("tab_w", [P, T], I32)
        tab_s = sb("tab_s", [P, T], U8)
        wb_w = sb("wb_w", [P, R], I32)
        wb_s = sb("wb_s", [P, R], U8)
        wgt = sb("wgt", [P, J], F32)
        x_planes = [sb("x%d" % i, [P, T], F32) for i in range(PACK)]
        wa_raw = sb("wa_raw", [P, PACK, R], F32, tag="wa_buffer")
        wd_raw = sb("wd_raw", [P, PACK, N], F32, tag="wd_buffer")
        res_sb = [sb("res%d" % side, [P, PACK, J // 2], F32) for side in range(2)]

        nc.vector.memset(wb_s[:].bitcast(I32), 0)

        x_rows = xT.rearrange("(p i) t -> p i t", i=PACK)
        wd_rows = wd.rearrange("(b t u) n -> t b u n", t=PACK, u=RUN)
        res_rows = res.rearrange("(p t) j -> p t j", t=PACK)
        out_rows = out_0.rearrange("(p t) j -> p t j", t=PACK)

        nc.sync.dma_start(tab_list[:], offs)
        for q in range(QUADRANTS):
            quadrant = tab_s[QUADRANT * q : QUADRANT * (q + 1), :].bitcast(I32)
            nc.sync.dma_start(quadrant, scale_rows(tab_scales, q).partition_broadcast(QUADRANT // PACK))
        nc.sync.dma_start(tab_w[:], words_of(tab_words))
        nc.sync.dma_start(wb_w[:], words_of(wb_words))
        nc.sync.dma_start(head_lists[:], offs2)
        for q in range(QUADRANTS):
            nc.sync.dma_start(live_rows(wb_s, q), scale_rows(wb_scales, q))
        nc.sync.dma_start(wgt[:], wgt2)
        for i in range(PACK):
            nc.sync.dma_start(x_planes[i][:], x_rows[:, i, :])
        nc.sync.dma_start(wa_raw[:], wa.rearrange("(p i) r -> p i r", i=PACK))
        for t in range(PACK):
            nc.sync.dma_start(wd_raw[:, t, :], wd_rows[t])
        for side in range(2):
            nc.sync.dma_start(res_sb[side][:], res_rows[:, :, side * (J // 2) : (side + 1) * (J // 2)])

        v_codes = sb("v_codes", [P, J], U32)
        v_scales = sb("v_scales", [P, J], U8)
        wb_codes = sb("wb_codes", [P, R], I32)
        wb_sc = sb("wb_sc", [P, R], U8)
        nc.vector.tensor_copy(v_scales[:], tab_s[:].indirect(tab_list[:]))
        nc.vector.tensor_copy(v_codes[:], tab_w[:].bitcast(U32).indirect(tab_list[:]))
        nc.vector.tensor_copy(
            wb_codes[:].rearrange("p (t b u) -> p t b u", t=PACK, u=RUN),
            wb_w[:].rearrange("p (b t u) -> p t b u", t=PACK, u=RUN),
        )
        nc.vector.tensor_copy(
            wb_sc[:].bitcast(I32).rearrange("p (t b u) -> p t b u", t=PACK, u=RUN // 4),
            wb_s[:].bitcast(I32).rearrange("p (b t u) -> p t b u", t=PACK, u=RUN // 4),
        )
        yb = []
        for c in range(J // BANK_COLS):
            cols = slice(c * BANK_COLS, (c + 1) * BANK_COLS)
            bank = bank_tile(4 + c % 4)
            project(bank, wb_codes, wb_sc, v_codes[:, cols], v_scales[:, cols])
            yb_c = sb("yb%d" % c, [P, BANK_COLS, PACK], F32)
            nc.scalar.copy(yb_c[:], bank[:].rearrange("p t j -> p j t"))
            yb.append(yb_c)

        picked = sb("picked", [P, PACK, J], F32)
        for i in range(PACK - 1):
            nc.vector.tensor_tensor(picked[:, i, :], x_planes[i][:].indirect(head_lists[:]), wgt[:], ALU.mult)

        wa_bf = sb("wa_bf", [P, PACK, P, PACK], BF16)
        wd_bf = sb("wd_bf", [P, PACK, P, PACK], BF16)
        wa_codes = sb("wa_codes", [P, R], U32)
        wa_sc = sb("wa_sc", [P, R], U8)
        wd_codes = sb("wd_codes", [P, N], U32)
        wd_sc = sb("wd_sc", [P, N], U8)
        out_codes = sb("out_codes", [P, J], U32)
        out_sc = sb("out_sc", [P, J], U8)
        xg_codes = sb("xg_codes", [P, J], U32)
        xg_sc = sb("xg_sc", [P, J], U8)
        h_bf = [sb("h_bf%d" % g, [P, GROUP, PACK], BF16) for g in range(GROUPS)]
        h_codes = [sb("h_codes%d" % g, [P, GROUP], U32) for g in range(GROUPS)]
        h_sc = [sb("h_sc%d" % g, [P, GROUP], U8) for g in range(GROUPS)]
        out_sb = [sb("out%d" % g, [P, PACK, GROUP], F32) for g in range(GROUPS)]
        out_bf = [sb("out_bf%d" % g, [P, GROUP, PACK], BF16) for g in range(GROUPS)]

        for start, stop in ((0, GROUP), (GROUP, 2 * GROUP), (2 * GROUP, J)):
            window = x_planes[PACK - 1][:].indirect(head_lists[:, start // PER_COL : stop // PER_COL])
            nc.vector.tensor_tensor(picked[:, PACK - 1, start:stop], window, wgt[:, start:stop], ALU.mult)

        xg0 = sb("xg0", [P, GROUP, PACK], BF16)
        weave(xg0[:], picked[:, :, group_cols(0)])
        wa_dealt = wa_raw[:].rearrange("p i (b t c e) -> p t b c i e", t=PACK, c=RUN // 2, e=2)
        for t in range(PACK):
            copy = nc.scalar.copy if t < PACK // 2 else nc.vector.tensor_copy
            copy(wa_bf[:, t].rearrange("p (b c e) i -> p b c i e", c=RUN // 2, e=2), wa_dealt[:, t])
        xg12 = sb("xg12", [P, 2, GROUP, PACK], BF16, tag="wa_buffer")
        weave(xg12[:, 0], picked[:, :, group_cols(1)])
        weave(xg12[:, 1], picked[:, :, group_cols(2)])
        nc.scalar.copy(
            wd_bf[:].rearrange("p (s e) m i -> p s m e i", e=2),
            wd_raw[:].rearrange("p i (m s e) -> p s m e i", s=2, e=2),
        )
        xg3 = sb("xg3", [P, GROUP, PACK], BF16, tag="wd_buffer")
        weave(xg3[:], picked[:, :, group_cols(3)])
        xg = [xg0[:], xg12[:, 0], xg12[:, 1], xg3[:]]

        def quantize_xg(g):
            quantize(xg_codes[:, group_cols(g)], xg_sc[:, group_cols(g)], xg[g].rearrange("p j i -> p (j i)"))

        def join(g, half, first_bank):
            cols = half_cols(g, half)
            bank = bank_tile(first_bank + half)
            project(bank, wa_codes, wa_sc, xg_codes[:, cols], xg_sc[:, cols])
            ya = bank[:].rearrange("p t j -> p j t")
            nc.vector.tensor_tensor(h_bf[g][:, half_cols(0, half), :], ya, yb[2 * g + half][:], ALU.max)

        def quantize_h(g):
            quantize(h_codes[g][:], h_sc[g][:], h_bf[g][:].rearrange("p j t -> p (j t)"))

        def second_layer(g, half, first_bank):
            local = half_cols(0, half)
            bank = bank_tile(first_bank + half)
            project(bank, wd_codes, wd_sc, h_codes[g][:, local], h_sc[g][:, local])
            residual = res_sb[g // 2][:, :, half_cols(g % 2, half)]
            nc.vector.tensor_tensor(out_sb[g][:, :, local], bank[:], residual, ALU.add)
            weave(out_bf[g][:, local, :], out_sb[g][:, :, local])
            if g == GROUPS - 1:
                nc.sync.dma_start(out_rows[:, :, half_cols(g, half)], out_sb[g][:, :, local])
            elif half == 1:
                nc.sync.dma_start(out_rows[:, :, group_cols(g)], out_sb[g][:])

        def hand_on(g):
            cols = group_cols(g)
            quantize(out_codes[:, cols], out_sc[:, cols], out_bf[g][:].rearrange("p j t -> p (j t)"))
            nc.sync.dma_start(words_of(out_1)[:, cols], out_codes[:, cols].bitcast(I32))

        quantize_xg(0)
        quantize(wa_codes[:], wa_sc[:], wa_bf[:].rearrange("p t m i -> p (t m i)"))
        quantize_xg(1)
        join(0, 0, 0)
        join(0, 1, 0)
        join(1, 0, 2)
        quantize_h(0)
        join(1, 1, 2)
        quantize_xg(2)
        quantize_h(1)
        quantize(wd_codes[:], wd_sc[:], wd_bf[:].rearrange("p t m i -> p (t m i)"))
        join(2, 0, 0)
        join(2, 1, 0)
        second_layer(0, 0, 4)
        quantize_h(2)
        second_layer(0, 1, 4)
        quantize_xg(3)
        second_layer(1, 0, 6)
        second_layer(1, 1, 6)
        hand_on(0)
        join(3, 0, 4)
        join(3, 1, 4)
        hand_on(1)
        quantize_h(3)
        second_layer(2, 0, 0)
        second_layer(2, 1, 0)
        second_layer(3, 0, 2)
        second_layer(3, 1, 2)
        hand_on(2)
        hand_on(3)

        for q in range(QUADRANTS):
            queue = nc.sync if q % 2 == 0 else nc.scalar
            queue.dma_start(scale_rows(out_2, q), live_rows(out_sc, q))
